import numpy as np
import ml_dtypes


def mxq(x, axis, fmt="e4m3"):
    dtype, down = {"e4m3": (ml_dtypes.float8_e4m3fn, 7), "e5m2": (ml_dtypes.float8_e5m2, 14)}[fmt]
    v = np.moveaxis(np.asarray(x, np.float32).astype(ml_dtypes.bfloat16).astype(np.float64), axis, -1)
    blocks = v.reshape(v.shape[:-1] + (-1, 32))
    amax = np.abs(blocks).max(-1, keepdims=True)
    byte = np.maximum(np.where(amax > 0, np.frexp(amax)[1] - 1 + 127, 0) - down, 1)
    scale = np.exp2(byte - 127.0)
    codes = (blocks / scale).astype(np.float32).astype(dtype).astype(np.float64)
    return np.moveaxis((codes * scale).reshape(v.shape), -1, axis)


WIDE = False


def mx_kscale(k):
    if not WIDE:
        return np.ones(k)
    levels = np.array([10, -10, 5, -5, 0])
    if k % 512:
        return np.exp2(np.random.permutation(np.resize(levels, k // 32))).repeat(32)
    a = np.empty((k // 512, 16))
    for p in range(k // 512):
        a[p, :8] = np.random.permutation(np.resize(levels, 8))
        for g in range(8):
            far = levels[np.abs(levels - a[p, g]) >= 10]
            a[p, g + 8] = far[np.random.randint(len(far))]
    return np.exp2(a.ravel()).repeat(32)


def f64(x):
    return np.asarray(x).astype(np.float64)


def striped(idx):
    return np.tile(idx.reshape(-1, 16).T, (8, 1)).astype(np.uint16)


def unstriped(offs):
    return offs[:16].T.reshape(-1).astype(np.int64)


def pack_weight(w):
    k, n = w.shape
    w = f64(np.asarray(w, np.float32).astype(ml_dtypes.bfloat16)).reshape(k // 32, 32, n)
    amax = np.abs(w).max(1)
    byte = np.clip(np.where(amax > 0, np.frexp(amax)[1] - 1 + 127 - 7, 1), 1, 254)
    scaled = (w * np.exp2(127.0 - byte)[:, None, :]).reshape(k, n).astype(np.float32)
    words = np.ascontiguousarray(scaled.reshape(k // 512, 128, 4, n).transpose(0, 1, 3, 2)).astype(ml_dtypes.float8_e4m3fn).view(np.uint8)
    return words, np.ascontiguousarray(byte.astype(np.uint8).reshape(k // 512, 16, n))


def unpack_weight(words, scales):
    g, p, n, _ = words.shape
    vals = np.ascontiguousarray(words).view(ml_dtypes.float8_e4m3fn).astype(np.float64) * np.repeat(np.exp2(scales.astype(np.float64) - 127.0), 8, axis=1)[..., None]
    return vals.transpose(0, 1, 3, 2).reshape(g * 512, n)


def gelu(v):
    return 0.5 * v * (1.0 + np.tanh(np.sqrt(2.0 / np.pi) * (v + 0.044715 * v**3)))


K, T, S, V, H, N = 1024, 2048, 768, 256, 512, 256


def setup_inputs():
    n = np.random.standard_normal
    s = mx_kscale(K)[:, None]
    u = mx_kscale(H)
    packed_w2 = pack_weight(n((H, N)) / np.sqrt(2 * H) / u[:, None])
    packed_w3 = pack_weight(n((H, N)) / np.sqrt(2 * H) / u[:, None])
    return {
        "xT": (n((K, T)) * s).astype(np.float32),
        "w1": (n((K, H)) / np.sqrt(K) / s * u).astype(np.float32),
        "w2_words": packed_w2[0],
        "w2_scales": packed_w2[1],
        "w3_words": packed_w3[0],
        "w3_scales": packed_w3[1],
        "offs": striped(np.random.permutation(T)[:S]),
    }


def reference(xT, w1, w2_words, w2_scales, w3_words, w3_scales, offs):
    xq = mxq(f64(xT)[:, unstriped(offs)], 0, "e4m3")
    h = gelu(mxq(f64(w1), 0, "e4m3").T @ xq)
    mean = (h[:, :V] + h[:, V:2 * V] + h[:, 2 * V:3 * V]) / 3
    dev = np.sqrt(((h[:, :V] - mean) ** 2 + (h[:, V:2 * V] - mean) ** 2 + (h[:, 2 * V:3 * V] - mean) ** 2) / 3)
    return unpack_weight(w2_words, w2_scales).T @ mxq(mean, 0, "e4m3") + unpack_weight(w3_words, w3_scales).T @ mxq(dev, 0, "e4m3")

@@ -1,0 +1,206 @@
+from contextlib import ExitStack
+
+import concourse.mybir as mybir
+
+K, T, S, V, H, N = 1024, 2048, 768, 256, 512, 256
+D = S // V
+FLOPS = 2 * K * H * S + 2 * 2 * H * N * V
+
+F32 = mybir.dt.float32
+BF16 = mybir.dt.bfloat16
+I32 = mybir.dt.int32
+U32 = mybir.dt.uint32
+U16 = mybir.dt.uint16
+U8 = mybir.dt.uint8
+FP8X4 = mybir.dt.float8_e4m3fn_x4
+ACT = mybir.ActivationFunctionType
+ALU = mybir.AluOpType
+
+P = 128
+PACK = 4
+PASSES = K // (P * PACK)
+HALF = 128
+HALVES = V // HALF
+LINE = 4
+SQRT_FLOOR = 2.0**-100
+
+STEADY_CHUNKS = ((1024, 768), (1024, 768))
+LAST_CHUNKS = ((1024, 768), (512, 384), (512, 192))
+
+
+def tile_picked_statpool_gelu_e_kernel(tc, xT, w1, w2_words, w2_scales, w3_words, w3_scales, offs, out):
+    nc = tc.nc
+    with ExitStack() as ctx:
+        keep = ctx.enter_context(tc.tile_pool(name="keep", bufs=1))
+        psum = ctx.enter_context(tc.psum_pool(name="psum", bufs=1))
+
+        def sbuf(shape, dtype, name):
+            return keep.tile(shape, dtype, name=name, align_bytes=64)
+
+        def quantise(values, width, name):
+            codes = sbuf([P, width], U32, name + "_codes")
+            scales = sbuf([P, width], U8, name + "_scales")
+            nc.vector.quantize_mx(out=codes[:].bitcast(FP8X4), scales=scales[:], in_=values)
+            return codes, scales
+
+        def multiply(acc, stationary, m_cols, moving, n_cols, start, stop):
+            nc.tensor.matmul_mx(
+                out=acc,
+                lhsT=stationary[0][:, m_cols].bitcast(FP8X4),
+                lhsT_scale=stationary[1][:, m_cols],
+                rhs=moving[0][:, n_cols].bitcast(FP8X4),
+                rhs_scale=moving[1][:, n_cols],
+                start=start,
+                stop=stop,
+            )
+
+        offsets = keep.tile([P, S // 16], U16, name="offsets")
+
+        warm_in = sbuf([P, 1], F32, "warm_in")
+        warm_out = sbuf([P, 1], F32, "warm_out")
+        nc.gpsimd.memset(warm_in[:], 0.0)
+        nc.scalar.activation(warm_out[:], warm_in[:], ACT.Gelu_apprx_tanh)
+
+        last_scales = []
+        for name in ("w2", "w3"):
+            scales = sbuf([P, N], U8, name + "_scales")
+            nc.gpsimd.memset(scales[:].bitcast(I32), 0)
+            last_scales.append(scales)
+
+        x_rows = xT.rearrange("(g p u j) t -> g u p j t", g=PASSES, p=P, u=2, j=2)
+        x_mx = {}
+        for g in range(PASSES):
+            picked = [sbuf([P, V, 2], U32, "picked%d%d" % (g, d)) for d in range(D)]
+            for u in range(2):
+                is_last = g == PASSES - 1 and u == 1
+                pairs = sbuf([P, T, 2], BF16, "pairs%d%d" % (g, u))
+                first = 0
+                for frames, scalar_share in LAST_CHUNKS if is_last else STEADY_CHUNKS:
+                    raw = sbuf([P, 2, frames], F32, "raw%d%d_%d" % (g, u, first))
+                    nc.sync.dma_start(out=raw[:], in_=x_rows[g, u][:, :, first : first + frames])
+                    if g == 0 and u == 0 and first == 0:
+                        nc.sync.dma_start(offsets[:], offs)
+                    for copy, lo, hi in ((nc.scalar.copy, 0, scalar_share), (nc.vector.tensor_copy, scalar_share, frames)):
+                        copy(
+                            pairs[:, first + lo : first + hi, :].rearrange("p (c i) j -> p c j i", i=LINE),
+                            raw[:, :, lo:hi].rearrange("p j (c i) -> p c j i", i=LINE),
+                        )
+                    first += frames
+                window = pairs[:].rearrange("p t j -> p (t j)").bitcast(U32)
+                for d in range(D):
+                    nc.vector.tensor_copy(picked[d][:, :, u], window.indirect(offsets[:, 16 * d : 16 * (d + 1)]))
+                    if u == 1 and d > 0:
+                        x_mx[g, d - 1] = quantise(picked[d - 1][:].rearrange("p v u -> p (v u)").bitcast(BF16), V, "x%d%d" % (g, d - 1))
+            x_mx[g, D - 1] = quantise(picked[D - 1][:].rearrange("p v u -> p (v u)").bitcast(BF16), V, "x%d%d" % (g, D - 1))
+
+        for r in range(6):
+            warm_bank = psum.tile([P, V], F32, name="warm_bank", tag="spare%d" % (r % 2))
+            multiply(warm_bank[:], x_mx[1, 0], slice(0, P), x_mx[0, r % D], slice(0, V), True, True)
+
+        w_rows = w1.rearrange("(g p j) c -> g p j c", g=PASSES, p=P, j=PACK)
+
+        def deal(copy, dealt, raw, raw_first, lo, hi):
+            copy(
+                dealt[:, :, lo:hi, :].rearrange("p t m j -> p m j t"),
+                raw[:, :, PACK * (lo - raw_first) : PACK * (hi - raw_first)].rearrange("p j (m t) -> p m j t", t=PACK),
+            )
+
+        dealt0 = sbuf([P, PACK, P, PACK], BF16, "dealt0")
+        w_raw0 = sbuf([P, PACK, H], F32, "w_raw0")
+        nc.sync.dma_start(out=w_raw0[:], in_=w_rows[0])
+        deal(nc.scalar.copy, dealt0, w_raw0, 0, 0, P)
+        dealt1 = sbuf([P, PACK, P, PACK], BF16, "dealt1")
+        w_raw1a = sbuf([P, PACK, H // 2], F32, "w_raw1a")
+        w_raw1b = sbuf([P, PACK, H // 2], F32, "w_raw1b")
+        nc.sync.dma_start(out=w_raw1a[:], in_=w_rows[1][:, :, : H // 2])
+        nc.sync.dma_start(out=w_raw1b[:], in_=w_rows[1][:, :, H // 2 :])
+        deal(nc.vector.tensor_copy, dealt1, w_raw1a, 0, 0, 64)
+        deal(nc.scalar.copy, dealt1, w_raw1b, 64, 64, 92)
+        deal(nc.vector.tensor_copy, dealt1, w_raw1b, 64, 92, 128)
+        w_first = quantise(dealt0[:].rearrange("p t m j -> p (t m j)"), H, "w1_0")
+        w_second = [quantise(dealt1[:, t].rearrange("p m j -> p (m j)"), P, "w1_1%d" % t) for t in range(PACK)]
+
+        last_weights = []
+        for name, words_in, scales_in, scales in (("w2", w2_words, w2_scales, last_scales[0]), ("w3", w3_words, w3_scales, last_scales[1])):
+            words = sbuf([P, N], U32, name + "_words")
+            nc.sync.dma_start(out=words[:].bitcast(I32), in_=words_in[0].rearrange("p n r -> p (n r)").bitcast(I32))
+            for q in range(4):
+                nc.sync.dma_start(out=scales[32 * q : 32 * q + 4, :].bitcast(I32), in_=scales_in[0, 4 * q : 4 * q + 4, :].bitcast(I32))
+            last_weights.append((words, scales))
+
+        banks = {}
+        for b in range(HALVES):
+            for d in range(D):
+                banks[b, d] = psum.tile([P, PACK, HALF], F32, name="bank%d%d" % (b, d), tag="bank%d%d" % (b, d))
+                multiply(banks[b, d][:, 0, :], w_first, slice(0, P), x_mx[0, d], slice(b * HALF, (b + 1) * HALF), True, False)
+
+        h = {}
+
+        def hidden(b, d):
+            segments = slice(b * HALF, (b + 1) * HALF)
+            for t in range(PACK):
+                if t > 0:
+                    multiply(banks[b, d][:, t, :], w_first, slice(t * P, (t + 1) * P), x_mx[0, d], segments, True, False)
+                multiply(banks[b, d][:, t, :], w_second[t], slice(0, P), x_mx[1, d], segments, False, True)
+            h[b, d] = sbuf([P, HALF * PACK], F32, "h%d%d" % (b, d))
+            nc.scalar.activation(h[b, d][:].rearrange("p (v t) -> p v t", t=PACK), banks[b, d][:].rearrange("p t v -> p v t"), ACT.Gelu_apprx_tanh)
+
+        def wide(name, dtype=F32):
+            return [sbuf([P, HALF * PACK], dtype, "%s%d" % (name, b)) for b in range(HALVES)]
+
+        pair_sum, pair_diff, third_diff, pair_sq, third_sq, sq_sum = (wide(n) for n in ("pair_sum", "pair_diff", "third_diff", "pair_sq", "third_sq", "sq_sum"))
+        mean, dev = wide("mean", BF16), wide("dev", BF16)
+
+        def contrasts(b):
+            nc.vector.tensor_tensor(pair_diff[b][:], h[b, 0][:], h[b, 1][:], ALU.subtract)
+            nc.vector.tensor_tensor(pair_sum[b][:], h[b, 0][:], h[b, 1][:], ALU.add)
+            nc.vector.scalar_tensor_tensor(third_diff[b][:], h[b, 2][:], -2.0, pair_sum[b][:], ALU.mult, ALU.add)
+
+        def add_squares(b):
+            nc.vector.scalar_tensor_tensor(sq_sum[b][:], pair_sq[b][:], SQRT_FLOOR, third_sq[b][:], ALU.max, ALU.add)
+
+        def make_mean(b):
+            nc.vector.scalar_tensor_tensor(mean[b][:], third_diff[b][:], 1.0 / 3.0, h[b, 2][:], ALU.mult, ALU.add)
+
+        def make_dev(b):
+            nc.scalar.activation(dev[b][:], sq_sum[b][:], ACT.Sqrt, scale=1.0 / 18.0)
+
+        acc_tags = (("spare0", "spare1"), ("bank00", "bank01"))
+        accs = {}
+
+        def mean_product(b):
+            mean_mx = quantise(mean[b][:], HALF, "mean%d" % b)
+            for r in range(2):
+                accs[b, r] = psum.tile([P, HALF], F32, name="acc%d%d" % (b, r), tag=acc_tags[b][r])
+                multiply(accs[b, r][:], last_weights[0], slice(r * P, (r + 1) * P), mean_mx, slice(0, HALF), True, False)
+
+        def dev_product(b):
+            dev_mx = quantise(dev[b][:], HALF, "dev%d" % b)
+            for r, copy, queue in ((0, nc.vector.tensor_copy, nc.sync), (1, nc.scalar.copy, nc.scalar)):
+                multiply(accs[b, r][:], last_weights[1], slice(r * P, (r + 1) * P), dev_mx, slice(0, HALF), False, True)
+                result = sbuf([P, HALF], F32, "result%d%d" % (b, r))
+                copy(result[:], accs[b, r][:])
+                queue.dma_start(out=out[r * P : (r + 1) * P, b * HALF : (b + 1) * HALF], in_=result[:])
+
+        def square(out_tile, in_tile, scale):
+            nc.scalar.activation(out_tile[:], in_tile[:], ACT.Square, scale=scale)
+
+        for b in range(HALVES):
+            for d in range(D):
+                hidden(b, d)
+        contrasts(0)
+        square(pair_sq[0], pair_diff[0], 3.0**0.5)
+        square(third_sq[0], third_diff[0], 1.0)
+        contrasts(1)
+        square(pair_sq[1], pair_diff[1], 3.0**0.5)
+        add_squares(0)
+        nc.vector.tensor_tensor(third_sq[1][:], third_diff[1][:], third_diff[1][:], ALU.mult)
+        make_dev(0)
+        make_mean(0)
+        add_squares(1)
+        make_dev(1)
+        make_mean(1)
+        mean_product(0)
+        mean_product(1)
+        dev_product(0)
+        dev_product(1)

@@ -1,6 +1,7 @@
 from contextlib import ExitStack
 
 import concourse.mybir as mybir
+from concourse.masks import make_identity
 
 K, T, S, V, H, N = 1024, 2048, 768, 256, 512, 256
 D = S // V
@@ -21,11 +22,14 @@ PACK = 4
 PASSES = K // (P * PACK)
 HALF = 128
 HALVES = V // HALF
+SIDES = 2
+SIDE = H // SIDES
+ROWS = SIDE // PACK
 LINE = 4
-SQRT_FLOOR = 2.0**-100
+SQRT_FLOOR = 2.0**-104
 
-STEADY_CHUNKS = ((1024, 768), (1024, 768))
-LAST_CHUNKS = ((1024, 768), (512, 384), (512, 192))
+STEADY_CHUNKS = ((1024, 640), (1024, 640))
+LAST_CHUNKS = ((1024, 640), (512, 320), (512, 160))
 
 
 def tile_picked_statpool_gelu_e_kernel(tc, xT, w1, w2_words, w2_scales, w3_words, w3_scales, offs, out):
@@ -34,11 +38,11 @@ def tile_picked_statpool_gelu_e_kernel(tc, xT, w1, w2_words, w2_scales, w3_words
         keep = ctx.enter_context(tc.tile_pool(name="keep", bufs=1))
         psum = ctx.enter_context(tc.psum_pool(name="psum", bufs=1))
 
-        def sbuf(shape, dtype, name):
-            return keep.tile(shape, dtype, name=name, align_bytes=64)
+        def sbuf(shape, dtype, name, tag=None):
+            return keep.tile(shape, dtype, name=name, tag=tag or name, align_bytes=64)
 
-        def quantise(values, width, name):
-            codes = sbuf([P, width], U32, name + "_codes")
+        def quantise(values, width, name, tag=None):
+            codes = sbuf([P, width], U32, name + "_codes", tag)
             scales = sbuf([P, width], U8, name + "_scales")
             nc.vector.quantize_mx(out=codes[:].bitcast(FP8X4), scales=scales[:], in_=values)
             return codes, scales
@@ -67,58 +71,74 @@ def tile_picked_statpool_gelu_e_kernel(tc, xT, w1, w2_words, w2_scales, w3_words
             nc.gpsimd.memset(scales[:].bitcast(I32), 0)
             last_scales.append(scales)
 
+        identity = sbuf([P, P], F32, "identity")
+        make_identity(nc, identity[:])
+
         x_rows = xT.rearrange("(g p u j) t -> g u p j t", g=PASSES, p=P, u=2, j=2)
-        x_mx = {}
-        for g in range(PASSES):
-            picked = [sbuf([P, V, 2], U32, "picked%d%d" % (g, d)) for d in range(D)]
-            for u in range(2):
-                is_last = g == PASSES - 1 and u == 1
-                pairs = sbuf([P, T, 2], BF16, "pairs%d%d" % (g, u))
-                first = 0
-                for frames, scalar_share in LAST_CHUNKS if is_last else STEADY_CHUNKS:
-                    raw = sbuf([P, 2, frames], F32, "raw%d%d_%d" % (g, u, first))
-                    nc.sync.dma_start(out=raw[:], in_=x_rows[g, u][:, :, first : first + frames])
-                    if g == 0 and u == 0 and first == 0:
-                        nc.sync.dma_start(offsets[:], offs)
-                    for copy, lo, hi in ((nc.scalar.copy, 0, scalar_share), (nc.vector.tensor_copy, scalar_share, frames)):
-                        copy(
-                            pairs[:, first + lo : first + hi, :].rearrange("p (c i) j -> p c j i", i=LINE),
-                            raw[:, :, lo:hi].rearrange("p j (c i) -> p c j i", i=LINE),
-                        )
-                    first += frames
-                window = pairs[:].rearrange("p t j -> p (t j)").bitcast(U32)
-                for d in range(D):
-                    nc.vector.tensor_copy(picked[d][:, :, u], window.indirect(offsets[:, 16 * d : 16 * (d + 1)]))
-                    if u == 1 and d > 0:
-                        x_mx[g, d - 1] = quantise(picked[d - 1][:].rearrange("p v u -> p (v u)").bitcast(BF16), V, "x%d%d" % (g, d - 1))
-            x_mx[g, D - 1] = quantise(picked[D - 1][:].rearrange("p v u -> p (v u)").bitcast(BF16), V, "x%d%d" % (g, D - 1))
-
-        for r in range(6):
-            warm_bank = psum.tile([P, V], F32, name="warm_bank", tag="spare%d" % (r % 2))
-            multiply(warm_bank[:], x_mx[1, 0], slice(0, P), x_mx[0, r % D], slice(0, V), True, True)
-
         w_rows = w1.rearrange("(g p j) c -> g p j c", g=PASSES, p=P, j=PACK)
+        x_mx, w_mx, picked, windows, w_bf16 = {}, {}, {}, {}, {}
 
-        def deal(copy, dealt, raw, raw_first, lo, hi):
-            copy(
-                dealt[:, :, lo:hi, :].rearrange("p t m j -> p m j t"),
-                raw[:, :, PACK * (lo - raw_first) : PACK * (hi - raw_first)].rearrange("p j (m t) -> p m j t", t=PACK),
-            )
+        def load_pairs(g, u, chunks):
+            pairs = sbuf([P, T, 2], BF16, "pairs%d%d" % (g, u))
+            first = 0
+            for frames, scalar_share in chunks:
+                raw = sbuf([P, 2, frames], F32, "raw%d%d_%d" % (g, u, first))
+                nc.sync.dma_start(out=raw[:], in_=x_rows[g, u][:, :, first : first + frames])
+                if g == 0 and u == 0 and first == 0:
+                    nc.sync.dma_start(offsets[:], offs)
+                for copy, lo, hi in ((nc.scalar.copy, 0, scalar_share), (nc.vector.tensor_copy, scalar_share, frames)):
+                    copy(pairs[:, first + lo : first + hi, :], raw[:, :, lo:hi].rearrange("p j c -> p c j"))
+                first += frames
+            windows[g, u] = pairs[:].rearrange("p t j -> p (t j)").bitcast(U32)
 
-        dealt0 = sbuf([P, PACK, P, PACK], BF16, "dealt0")
-        w_raw0 = sbuf([P, PACK, H], F32, "w_raw0")
-        nc.sync.dma_start(out=w_raw0[:], in_=w_rows[0])
-        deal(nc.scalar.copy, dealt0, w_raw0, 0, 0, P)
-        dealt1 = sbuf([P, PACK, P, PACK], BF16, "dealt1")
-        w_raw1a = sbuf([P, PACK, H // 2], F32, "w_raw1a")
-        w_raw1b = sbuf([P, PACK, H // 2], F32, "w_raw1b")
-        nc.sync.dma_start(out=w_raw1a[:], in_=w_rows[1][:, :, : H // 2])
-        nc.sync.dma_start(out=w_raw1b[:], in_=w_rows[1][:, :, H // 2 :])
-        deal(nc.vector.tensor_copy, dealt1, w_raw1a, 0, 0, 64)
-        deal(nc.scalar.copy, dealt1, w_raw1b, 64, 64, 92)
-        deal(nc.vector.tensor_copy, dealt1, w_raw1b, 64, 92, 128)
-        w_first = quantise(dealt0[:].rearrange("p t m j -> p (t m j)"), H, "w1_0")
-        w_second = [quantise(dealt1[:, t].rearrange("p m j -> p (m j)"), P, "w1_1%d" % t) for t in range(PACK)]
+        def gather(g, u, d):
+            if u == 0:
+                picked[g, d] = sbuf([P, V, 2], U32, "picked%d%d" % (g, d))
+            nc.vector.tensor_copy(picked[g, d][:, :, u], windows[g, u].indirect(offsets[:, 16 * d : 16 * (d + 1)]))
+
+        def quantise_x(g, d, tag=None):
+            x_mx[g, d] = quantise(picked[g, d][:].rearrange("p v u -> p (v u)").bitcast(BF16), V, "x%d%d" % (g, d), tag)
+
+        def load_w(c, g, copy):
+            raw = sbuf([P, PACK, SIDE], F32, "w_raw%d%d" % (c, g))
+            nc.sync.dma_start(out=raw[:], in_=w_rows[g][:, :, c * SIDE : (c + 1) * SIDE])
+            w_bf16[c, g] = sbuf([P, SIDE, PACK], BF16, "w_bf16_%d%d" % (c, g))
+            copy(w_bf16[c, g][:].rearrange("p (n i) j -> p n j i", i=LINE), raw[:].rearrange("p j (n i) -> p n j i", i=LINE))
+
+        def quantise_w(c, g):
+            w_mx[c, g] = quantise(w_bf16[c, g][:].rearrange("p n j -> p (n j)"), SIDE, "w1_%d%d" % (c, g))
+
+        for g, u in ((0, 0), (0, 1), (1, 0)):
+            load_pairs(g, u, STEADY_CHUNKS)
+            for d in range(D):
+                gather(g, u, d)
+            if u == 1:
+                for d in range(D):
+                    quantise_x(g, d)
+        load_pairs(1, 1, LAST_CHUNKS)
+        load_w(0, 0, nc.scalar.copy)
+        load_w(0, 1, nc.scalar.copy)
+        load_w(1, 0, nc.scalar.copy)
+        def bank(number, shape):
+            return psum.tile(shape, F32, name="bank%d" % number, tag="bank%d" % number)
+
+        def keep_clock(number, passes):
+            for r in range(passes):
+                multiply(bank(number, [P, V])[:], x_mx[1, 0], slice(0, P), x_mx[0, r % D], slice(0, V), True, True)
+
+        gather(1, 1, 0)
+        quantise_x(1, 0)
+        keep_clock(6, 2)
+        keep_clock(7, 2)
+        gather(1, 1, 1)
+        gather(1, 1, 2)
+        quantise_w(0, 0)
+        quantise_w(0, 1)
+        quantise_x(1, 1, "w_bf16_01")
+        quantise_x(1, 2)
+        quantise_w(1, 0)
+        load_w(1, 1, nc.vector.tensor_copy)
+        quantise_w(1, 1)
 
         last_weights = []
         for name, words_in, scales_in, scales in (("w2", w2_words, w2_scales, last_scales[0]), ("w3", w3_words, w3_scales, last_scales[1])):
@@ -128,79 +148,91 @@ def tile_picked_statpool_gelu_e_kernel(tc, xT, w1, w2_words, w2_scales, w3_words
                 nc.sync.dma_start(out=scales[32 * q : 32 * q + 4, :].bitcast(I32), in_=scales_in[0, 4 * q : 4 * q + 4, :].bitcast(I32))
             last_weights.append((words, scales))
 
-        banks = {}
-        for b in range(HALVES):
-            for d in range(D):
-                banks[b, d] = psum.tile([P, PACK, HALF], F32, name="bank%d%d" % (b, d), tag="bank%d%d" % (b, d))
-                multiply(banks[b, d][:, 0, :], w_first, slice(0, P), x_mx[0, d], slice(b * HALF, (b + 1) * HALF), True, False)
+        def joint(name, tag=None):
+            return sbuf([P, HALVES, PACK, SIDES, ROWS], F32, name, tag)
 
-        h = {}
+        def side(tile, c):
+            return tile[:, :, :, c, :].rearrange("p b t m -> p (b t) m")
 
-        def hidden(b, d):
-            segments = slice(b * HALF, (b + 1) * HALF)
+        h = [joint("h%d" % d) for d in range(D)]
+
+        def first_product(acc, c, d, b, g):
+            multiply(acc, x_mx[g, d], slice(b * HALF, (b + 1) * HALF), w_mx[c, g], slice(0, SIDE), g == 0, g == PASSES - 1)
+
+        early = {(d, b): bank(HALVES * d + b, [P, SIDE]) for d in range(D) for b in range(HALVES)}
+        for (d, b), acc in early.items():
+            for g in range(PASSES):
+                first_product(acc[:], 0, d, b, g)
+            nc.scalar.activation(h[d][:, b, :, 0, :], acc[:].rearrange("p (m t) -> p t m", t=PACK), ACT.Gelu_apprx_tanh)
+        late = [bank(number, [P, HALVES, SIDE]) for number in (6, 7, 0)]
+        for d in range(D):
+            for b in range(HALVES):
+                for g in range(PASSES):
+                    first_product(late[d][:, b, :], 1, d, b, g)
+            nc.scalar.activation(h[d][:, :, :, 1, :], late[d][:].rearrange("p b (m t) -> p b t m", t=PACK), ACT.Gelu_apprx_tanh)
+
+        keep_clock(6, 1)
+        keep_clock(7, 2)
+
+        pair_sum, pair_sq, third_sq = joint("pair_sum"), joint("pair_sq", "w1_11_codes"), joint("third_sq", "x12_codes")
+
+        def per_side(name):
+            return [sbuf([P, HALVES * PACK, ROWS], F32, "%s%d" % (name, c)) for c in range(SIDES)]
+
+        pair_diff, third_diff = per_side("pair_diff"), per_side("third_diff")
+
+        def contrasts(c):
+            nc.vector.tensor_tensor(side(pair_sum, c), side(h[0], c), side(h[1], c), ALU.add)
+            nc.vector.tensor_tensor(pair_diff[c][:], side(h[0], c), side(h[1], c), ALU.subtract)
+            nc.vector.scalar_tensor_tensor(third_diff[c][:], side(h[2], c), -2.0, side(pair_sum, c), ALU.mult, ALU.add)
+
+        def turn_and_add(b, terms, number):
+            turned = bank(number, [P, PACK, HALF])
             for t in range(PACK):
-                if t > 0:
-                    multiply(banks[b, d][:, t, :], w_first, slice(t * P, (t + 1) * P), x_mx[0, d], segments, True, False)
-                multiply(banks[b, d][:, t, :], w_second[t], slice(0, P), x_mx[1, d], segments, False, True)
-            h[b, d] = sbuf([P, HALF * PACK], F32, "h%d%d" % (b, d))
-            nc.scalar.activation(h[b, d][:].rearrange("p (v t) -> p v t", t=PACK), banks[b, d][:].rearrange("p t v -> p v t"), ACT.Gelu_apprx_tanh)
+                for n, term in enumerate(terms):
+                    nc.tensor.matmul(turned[:, t, :], term[:, b, t].rearrange("p c m -> p (c m)"), identity[:], start=n == 0, stop=n == len(terms) - 1, is_transpose=True)
+            return turned[:].rearrange("p t v -> p v t")
 
-        def wide(name, dtype=F32):
-            return [sbuf([P, HALF * PACK], dtype, "%s%d" % (name, b)) for b in range(HALVES)]
+        for c in range(SIDES):
+            contrasts(c)
+        nc.scalar.activation(side(pair_sq, 0), pair_diff[0][:], ACT.Square, scale=3.0**0.5)
+        nc.scalar.activation(side(third_sq, 0), third_diff[0][:], ACT.Square)
+        root_table = sbuf([P, 1], F32, "root_table")
+        nc.scalar.activation(root_table[:], third_sq[:, 0, 0, 0, 0:1], ACT.Sqrt, bias=SQRT_FLOOR)
+        sums = [turn_and_add(b, (h[2], pair_sum), 1 + b) for b in range(HALVES)]
+        for b in range(HALVES):
+            rows = slice(b * PACK, (b + 1) * PACK)
+            nc.vector.scalar_tensor_tensor(pair_sq[:, b, :, 1, :], pair_diff[1][:, rows], 3.0, pair_diff[1][:, rows], ALU.mult, ALU.mult)
+            nc.vector.tensor_tensor(third_sq[:, b, :, 1, :], third_diff[1][:, rows], third_diff[1][:, rows], ALU.mult)
+        squares = [turn_and_add(b, (pair_sq, third_sq), 3 + b) for b in range(HALVES)]
 
-        pair_sum, pair_diff, third_diff, pair_sq, third_sq, sq_sum = (wide(n) for n in ("pair_sum", "pair_diff", "third_diff", "pair_sq", "third_sq", "sq_sum"))
-        mean, dev = wide("mean", BF16), wide("dev", BF16)
+        mean = [sbuf([P, HALF, PACK], BF16, "mean%d" % b, tag) for b, tag in enumerate(("third_diff1", "pair_diff1"))]
+        dev = [sbuf([P, HALF, PACK], BF16, "dev%d" % b) for b in range(HALVES)]
+        for b in range(HALVES):
+            nc.scalar.activation(dev[b][:], squares[b], ACT.Sqrt, bias=SQRT_FLOOR, scale=1.0 / 18.0)
+            nc.vector.tensor_scalar(mean[b][:], sums[b], 1.0 / 3.0, None, ALU.mult)
 
-        def contrasts(b):
-            nc.vector.tensor_tensor(pair_diff[b][:], h[b, 0][:], h[b, 1][:], ALU.subtract)
-            nc.vector.tensor_tensor(pair_sum[b][:], h[b, 0][:], h[b, 1][:], ALU.add)
-            nc.vector.scalar_tensor_tensor(third_diff[b][:], h[b, 2][:], -2.0, pair_sum[b][:], ALU.mult, ALU.add)
-
-        def add_squares(b):
-            nc.vector.scalar_tensor_tensor(sq_sum[b][:], pair_sq[b][:], SQRT_FLOOR, third_sq[b][:], ALU.max, ALU.add)
-
-        def make_mean(b):
-            nc.vector.scalar_tensor_tensor(mean[b][:], third_diff[b][:], 1.0 / 3.0, h[b, 2][:], ALU.mult, ALU.add)
-
-        def make_dev(b):
-            nc.scalar.activation(dev[b][:], sq_sum[b][:], ACT.Sqrt, scale=1.0 / 18.0)
-
-        acc_tags = (("spare0", "spare1"), ("bank00", "bank01"))
+        acc_banks = ((5, 6), (7, 0))
+        out_copies = ((nc.scalar.copy, nc.scalar.copy), (nc.vector.tensor_copy, nc.scalar.copy))
         accs = {}
 
         def mean_product(b):
-            mean_mx = quantise(mean[b][:], HALF, "mean%d" % b)
+            mean_mx = quantise(mean[b][:].rearrange("p v t -> p (v t)"), HALF, "mean%d" % b)
             for r in range(2):
-                accs[b, r] = psum.tile([P, HALF], F32, name="acc%d%d" % (b, r), tag=acc_tags[b][r])
+                accs[b, r] = bank(acc_banks[b][r], [P, HALF])
                 multiply(accs[b, r][:], last_weights[0], slice(r * P, (r + 1) * P), mean_mx, slice(0, HALF), True, False)
 
         def dev_product(b):
-            dev_mx = quantise(dev[b][:], HALF, "dev%d" % b)
-            for r, copy, queue in ((0, nc.vector.tensor_copy, nc.sync), (1, nc.scalar.copy, nc.scalar)):
+            dev_mx = quantise(dev[b][:].rearrange("p v t -> p (v t)"), HALF, "dev%d" % b)
+            for r in range(2):
                 multiply(accs[b, r][:], last_weights[1], slice(r * P, (r + 1) * P), dev_mx, slice(0, HALF), False, True)
-                result = sbuf([P, HALF], F32, "result%d%d" % (b, r))
-                copy(result[:], accs[b, r][:])
-                queue.dma_start(out=out[r * P : (r + 1) * P, b * HALF : (b + 1) * HALF], in_=result[:])
 
-        def square(out_tile, in_tile, scale):
-            nc.scalar.activation(out_tile[:], in_tile[:], ACT.Square, scale=scale)
+        def store(b):
+            result = sbuf([P, 2, HALF], F32, "result%d" % b)
+            for r in range(2):
+                out_copies[b][r](result[:, r, :], accs[b, r][:])
+            nc.sync.dma_start(out=out.rearrange("(r p) v -> p r v", p=P)[:, :, b * HALF : (b + 1) * HALF], in_=result[:])
 
-        for b in range(HALVES):
-            for d in range(D):
-                hidden(b, d)
-        contrasts(0)
-        square(pair_sq[0], pair_diff[0], 3.0**0.5)
-        square(third_sq[0], third_diff[0], 1.0)
-        contrasts(1)
-        square(pair_sq[1], pair_diff[1], 3.0**0.5)
-        add_squares(0)
-        nc.vector.tensor_tensor(third_sq[1][:], third_diff[1][:], third_diff[1][:], ALU.mult)
-        make_dev(0)
-        make_mean(0)
-        add_squares(1)
-        make_dev(1)
-        make_mean(1)
-        mean_product(0)
-        mean_product(1)
-        dev_product(0)
-        dev_product(1)
+        for stage in (mean_product, dev_product, store):
+            for b in range(HALVES):
+                stage(b)

from contextlib import ExitStack

import concourse.mybir as mybir
from concourse.masks import make_identity

K, T, S, V, H, N = 1024, 2048, 768, 256, 512, 256
D = S // V
FLOPS = 2 * K * H * S + 2 * 2 * H * N * V

F32 = mybir.dt.float32
BF16 = mybir.dt.bfloat16
I32 = mybir.dt.int32
U32 = mybir.dt.uint32
U16 = mybir.dt.uint16
U8 = mybir.dt.uint8
FP8X4 = mybir.dt.float8_e4m3fn_x4
ACT = mybir.ActivationFunctionType
ALU = mybir.AluOpType

P = 128
PACK = 4
PASSES = K // (P * PACK)
HALF = 128
HALVES = V // HALF
SIDES = 2
SIDE = H // SIDES
ROWS = SIDE // PACK
LINE = 4
SQRT_FLOOR = 2.0**-104

STEADY_CHUNKS = ((1024, 640), (1024, 640))
LAST_CHUNKS = ((1024, 640), (512, 320), (512, 160))


def tile_picked_statpool_gelu_e_kernel(tc, xT, w1, w2_words, w2_scales, w3_words, w3_scales, offs, out):
    nc = tc.nc
    with ExitStack() as ctx:
        keep = ctx.enter_context(tc.tile_pool(name="keep", bufs=1))
        psum = ctx.enter_context(tc.psum_pool(name="psum", bufs=1))

        def sbuf(shape, dtype, name, tag=None):
            return keep.tile(shape, dtype, name=name, tag=tag or name, align_bytes=64)

        def quantise(values, width, name, tag=None):
            codes = sbuf([P, width], U32, name + "_codes", tag)
            scales = sbuf([P, width], U8, name + "_scales")
            nc.vector.quantize_mx(out=codes[:].bitcast(FP8X4), scales=scales[:], in_=values)
            return codes, scales

        def multiply(acc, stationary, m_cols, moving, n_cols, start, stop):
            nc.tensor.matmul_mx(
                out=acc,
                lhsT=stationary[0][:, m_cols].bitcast(FP8X4),
                lhsT_scale=stationary[1][:, m_cols],
                rhs=moving[0][:, n_cols].bitcast(FP8X4),
                rhs_scale=moving[1][:, n_cols],
                start=start,
                stop=stop,
            )

        offsets = keep.tile([P, S // 16], U16, name="offsets")

        warm_in = sbuf([P, 1], F32, "warm_in")
        warm_out = sbuf([P, 1], F32, "warm_out")
        nc.gpsimd.memset(warm_in[:], 0.0)
        nc.scalar.activation(warm_out[:], warm_in[:], ACT.Gelu_apprx_tanh)

        last_scales = []
        for name in ("w2", "w3"):
            scales = sbuf([P, N], U8, name + "_scales")
            nc.gpsimd.memset(scales[:].bitcast(I32), 0)
            last_scales.append(scales)

        identity = sbuf([P, P], F32, "identity")
        make_identity(nc, identity[:])

        x_rows = xT.rearrange("(g p u j) t -> g u p j t", g=PASSES, p=P, u=2, j=2)
        w_rows = w1.rearrange("(g p j) c -> g p j c", g=PASSES, p=P, j=PACK)
        x_mx, w_mx, picked, windows, w_bf16 = {}, {}, {}, {}, {}

        def load_pairs(g, u, chunks):
            pairs = sbuf([P, T, 2], BF16, "pairs%d%d" % (g, u))
            first = 0
            for frames, scalar_share in chunks:
                raw = sbuf([P, 2, frames], F32, "raw%d%d_%d" % (g, u, first))
                nc.sync.dma_start(out=raw[:], in_=x_rows[g, u][:, :, first : first + frames])
                if g == 0 and u == 0 and first == 0:
                    nc.sync.dma_start(offsets[:], offs)
                for copy, lo, hi in ((nc.scalar.copy, 0, scalar_share), (nc.vector.tensor_copy, scalar_share, frames)):
                    copy(pairs[:, first + lo : first + hi, :], raw[:, :, lo:hi].rearrange("p j c -> p c j"))
                first += frames
            windows[g, u] = pairs[:].rearrange("p t j -> p (t j)").bitcast(U32)

        def gather(g, u, d):
            if u == 0:
                picked[g, d] = sbuf([P, V, 2], U32, "picked%d%d" % (g, d))
            nc.vector.tensor_copy(picked[g, d][:, :, u], windows[g, u].indirect(offsets[:, 16 * d : 16 * (d + 1)]))

        def quantise_x(g, d, tag=None):
            x_mx[g, d] = quantise(picked[g, d][:].rearrange("p v u -> p (v u)").bitcast(BF16), V, "x%d%d" % (g, d), tag)

        def load_w(c, g, copy):
            raw = sbuf([P, PACK, SIDE], F32, "w_raw%d%d" % (c, g))
            nc.sync.dma_start(out=raw[:], in_=w_rows[g][:, :, c * SIDE : (c + 1) * SIDE])
            w_bf16[c, g] = sbuf([P, SIDE, PACK], BF16, "w_bf16_%d%d" % (c, g))
            copy(w_bf16[c, g][:].rearrange("p (n i) j -> p n j i", i=LINE), raw[:].rearrange("p j (n i) -> p n j i", i=LINE))

        def quantise_w(c, g):
            w_mx[c, g] = quantise(w_bf16[c, g][:].rearrange("p n j -> p (n j)"), SIDE, "w1_%d%d" % (c, g))

        for g, u in ((0, 0), (0, 1), (1, 0)):
            load_pairs(g, u, STEADY_CHUNKS)
            for d in range(D):
                gather(g, u, d)
            if u == 1:
                for d in range(D):
                    quantise_x(g, d)
        load_pairs(1, 1, LAST_CHUNKS)
        load_w(0, 0, nc.scalar.copy)
        load_w(0, 1, nc.scalar.copy)
        load_w(1, 0, nc.scalar.copy)
        def bank(number, shape):
            return psum.tile(shape, F32, name="bank%d" % number, tag="bank%d" % number)

        def keep_clock(number, passes):
            for r in range(passes):
                multiply(bank(number, [P, V])[:], x_mx[1, 0], slice(0, P), x_mx[0, r % D], slice(0, V), True, True)

        gather(1, 1, 0)
        quantise_x(1, 0)
        keep_clock(6, 2)
        keep_clock(7, 2)
        gather(1, 1, 1)
        gather(1, 1, 2)
        quantise_w(0, 0)
        quantise_w(0, 1)
        quantise_x(1, 1, "w_bf16_01")
        quantise_x(1, 2)
        quantise_w(1, 0)
        load_w(1, 1, nc.vector.tensor_copy)
        quantise_w(1, 1)

        last_weights = []
        for name, words_in, scales_in, scales in (("w2", w2_words, w2_scales, last_scales[0]), ("w3", w3_words, w3_scales, last_scales[1])):
            words = sbuf([P, N], U32, name + "_words")
            nc.sync.dma_start(out=words[:].bitcast(I32), in_=words_in[0].rearrange("p n r -> p (n r)").bitcast(I32))
            for q in range(4):
                nc.sync.dma_start(out=scales[32 * q : 32 * q + 4, :].bitcast(I32), in_=scales_in[0, 4 * q : 4 * q + 4, :].bitcast(I32))
            last_weights.append((words, scales))

        def joint(name, tag=None):
            return sbuf([P, HALVES, PACK, SIDES, ROWS], F32, name, tag)

        def side(tile, c):
            return tile[:, :, :, c, :].rearrange("p b t m -> p (b t) m")

        h = [joint("h%d" % d) for d in range(D)]

        def first_product(acc, c, d, b, g):
            multiply(acc, x_mx[g, d], slice(b * HALF, (b + 1) * HALF), w_mx[c, g], slice(0, SIDE), g == 0, g == PASSES - 1)

        early = {(d, b): bank(HALVES * d + b, [P, SIDE]) for d in range(D) for b in range(HALVES)}
        for (d, b), acc in early.items():
            for g in range(PASSES):
                first_product(acc[:], 0, d, b, g)
            nc.scalar.activation(h[d][:, b, :, 0, :], acc[:].rearrange("p (m t) -> p t m", t=PACK), ACT.Gelu_apprx_tanh)
        late = [bank(number, [P, HALVES, SIDE]) for number in (6, 7, 0)]
        for d in range(D):
            for b in range(HALVES):
                for g in range(PASSES):
                    first_product(late[d][:, b, :], 1, d, b, g)
            nc.scalar.activation(h[d][:, :, :, 1, :], late[d][:].rearrange("p b (m t) -> p b t m", t=PACK), ACT.Gelu_apprx_tanh)

        keep_clock(6, 1)
        keep_clock(7, 2)

        pair_sum, pair_sq, third_sq = joint("pair_sum"), joint("pair_sq", "w1_11_codes"), joint("third_sq", "x12_codes")

        def per_side(name):
            return [sbuf([P, HALVES * PACK, ROWS], F32, "%s%d" % (name, c)) for c in range(SIDES)]

        pair_diff, third_diff = per_side("pair_diff"), per_side("third_diff")

        def contrasts(c):
            nc.vector.tensor_tensor(side(pair_sum, c), side(h[0], c), side(h[1], c), ALU.add)
            nc.vector.tensor_tensor(pair_diff[c][:], side(h[0], c), side(h[1], c), ALU.subtract)
            nc.vector.scalar_tensor_tensor(third_diff[c][:], side(h[2], c), -2.0, side(pair_sum, c), ALU.mult, ALU.add)

        def turn_and_add(b, terms, number):
            turned = bank(number, [P, PACK, HALF])
            for t in range(PACK):
                for n, term in enumerate(terms):
                    nc.tensor.matmul(turned[:, t, :], term[:, b, t].rearrange("p c m -> p (c m)"), identity[:], start=n == 0, stop=n == len(terms) - 1, is_transpose=True)
            return turned[:].rearrange("p t v -> p v t")

        for c in range(SIDES):
            contrasts(c)
        nc.scalar.activation(side(pair_sq, 0), pair_diff[0][:], ACT.Square, scale=3.0**0.5)
        nc.scalar.activation(side(third_sq, 0), third_diff[0][:], ACT.Square)
        root_table = sbuf([P, 1], F32, "root_table")
        nc.scalar.activation(root_table[:], third_sq[:, 0, 0, 0, 0:1], ACT.Sqrt, bias=SQRT_FLOOR)
        sums = [turn_and_add(b, (h[2], pair_sum), 1 + b) for b in range(HALVES)]
        for b in range(HALVES):
            rows = slice(b * PACK, (b + 1) * PACK)
            nc.vector.scalar_tensor_tensor(pair_sq[:, b, :, 1, :], pair_diff[1][:, rows], 3.0, pair_diff[1][:, rows], ALU.mult, ALU.mult)
            nc.vector.tensor_tensor(third_sq[:, b, :, 1, :], third_diff[1][:, rows], third_diff[1][:, rows], ALU.mult)
        squares = [turn_and_add(b, (pair_sq, third_sq), 3 + b) for b in range(HALVES)]

        mean = [sbuf([P, HALF, PACK], BF16, "mean%d" % b, tag) for b, tag in enumerate(("third_diff1", "pair_diff1"))]
        dev = [sbuf([P, HALF, PACK], BF16, "dev%d" % b) for b in range(HALVES)]
        for b in range(HALVES):
            nc.scalar.activation(dev[b][:], squares[b], ACT.Sqrt, bias=SQRT_FLOOR, scale=1.0 / 18.0)
            nc.vector.tensor_scalar(mean[b][:], sums[b], 1.0 / 3.0, None, ALU.mult)

        acc_banks = ((5, 6), (7, 0))
        out_copies = ((nc.scalar.copy, nc.scalar.copy), (nc.vector.tensor_copy, nc.scalar.copy))
        accs = {}

        def mean_product(b):
            mean_mx = quantise(mean[b][:].rearrange("p v t -> p (v t)"), HALF, "mean%d" % b)
            for r in range(2):
                accs[b, r] = bank(acc_banks[b][r], [P, HALF])
                multiply(accs[b, r][:], last_weights[0], slice(r * P, (r + 1) * P), mean_mx, slice(0, HALF), True, False)

        def dev_product(b):
            dev_mx = quantise(dev[b][:].rearrange("p v t -> p (v t)"), HALF, "dev%d" % b)
            for r in range(2):
                multiply(accs[b, r][:], last_weights[1], slice(r * P, (r + 1) * P), dev_mx, slice(0, HALF), False, True)

        def store(b):
            result = sbuf([P, 2, HALF], F32, "result%d" % b)
            for r in range(2):
                out_copies[b][r](result[:, r, :], accs[b, r][:])
            nc.sync.dma_start(out=out.rearrange("(r p) v -> p r v", p=P)[:, :, b * HALF : (b + 1) * HALF], in_=result[:])

        for stage in (mean_product, dev_product, store):
            for b in range(HALVES):
                stage(b)
